import numpy as np
import ml_dtypes


def mxq(x, axis, fmt="e4m3"):
    dtype, down = {"e4m3": (ml_dtypes.float8_e4m3fn, 7), "e5m2": (ml_dtypes.float8_e5m2, 14)}[fmt]
    v = np.moveaxis(np.asarray(x, np.float32).astype(ml_dtypes.bfloat16).astype(np.float64), axis, -1)
    blocks = v.reshape(v.shape[:-1] + (-1, 32))
    amax = np.abs(blocks).max(-1, keepdims=True)
    byte = np.maximum(np.where(amax > 0, np.frexp(amax)[1] - 1 + 127, 0) - down, 1)
    scale = np.exp2(byte - 127.0)
    codes = (blocks / scale).astype(np.float32).astype(dtype).astype(np.float64)
    return np.moveaxis((codes * scale).reshape(v.shape), -1, axis)


WIDE = False


def mx_kscale(k):
    if not WIDE:
        return np.ones(k)
    levels = np.array([10, -10, 5, -5, 0])
    if k % 512:
        return np.exp2(np.random.permutation(np.resize(levels, k // 32))).repeat(32)
    a = np.empty((k // 512, 16))
    for p in range(k // 512):
        a[p, :8] = np.random.permutation(np.resize(levels, 8))
        for g in range(8):
            far = levels[np.abs(levels - a[p, g]) >= 10]
            a[p, g + 8] = far[np.random.randint(len(far))]
    return np.exp2(a.ravel()).repeat(32)


def f64(x):
    return np.asarray(x).astype(np.float64)


def striped8(idx):
    return np.asarray(idx).reshape(8, -1, 16).transpose(0, 2, 1).reshape(128, -1).astype(np.uint16)


def unstriped8(offs):
    return offs.reshape(8, 16, -1).transpose(0, 2, 1).reshape(8, -1).astype(np.int64)


def pick8(x, idx, run):
    r = np.arange(len(x))
    return x[r[:, None], idx[r % (8 * run) // run]]


E2M1 = np.array([0.0, 0.5, 1.0, 1.5, 2.0, 3.0, 4.0, 6.0, -0.0, -0.5, -1.0, -1.5, -2.0, -3.0, -4.0, -6.0])


def pack_weight(w, fmt):
    k, n = w.shape
    w = f64(np.asarray(w, np.float32).astype(ml_dtypes.bfloat16)).reshape(k // 32, 32, n)
    amax = np.abs(w).max(1)
    if fmt == "e4m3":
        byte = np.frexp(amax)[1] - 1 + 127 - 7
    else:
        mant, ex = np.frexp(amax / 6.0)
        byte = np.where(mant > 0.5, ex, ex - 1) + 127
    byte = np.clip(np.where(amax > 0, byte, 1), 1, 254)
    scaled = (w * np.exp2(127.0 - byte)[:, None, :]).reshape(k, n).astype(np.float32)
    by_word = np.ascontiguousarray(scaled.reshape(k // 512, 128, 4, n).transpose(0, 1, 3, 2))
    if fmt == "e4m3":
        words = by_word.astype(ml_dtypes.float8_e4m3fn).view(np.uint8)
    else:
        c = by_word.astype(ml_dtypes.float4_e2m1fn).view(np.uint8) & 0xF
        words = (c[..., 0::2] | (c[..., 1::2] << 4)).reshape(k // 512, 128, 2 * n)
    return np.ascontiguousarray(words), np.ascontiguousarray(byte.astype(np.uint8).reshape(k // 512, 16, n))


def unpack_weight(words, scales, fmt):
    g, _, n = scales.shape
    words = np.ascontiguousarray(words).reshape(g, 128, n, -1)
    if fmt == "e4m3":
        vals = words.view(ml_dtypes.float8_e4m3fn).astype(np.float64)
    else:
        nib = np.empty((g, 128, n, 4), np.uint8)
        nib[..., 0::2] = words & 0xF
        nib[..., 1::2] = words >> 4
        vals = E2M1[nib]
    vals = vals * np.repeat(np.exp2(scales.astype(np.float64) - 127.0), 8, axis=1)[..., None]
    return vals.transpose(0, 1, 3, 2).reshape(g * 512, n)


D, T, I, Q = 512, 1024, 512, 128


def setup_inputs():
    n = np.random.standard_normal
    idx = np.stack([np.random.permutation(T)[:I] for _ in range(8)])
    idx2 = np.stack([np.random.permutation(T)[:I] for _ in range(8)])
    idx3 = np.stack([np.random.permutation(T)[:I] for _ in range(8)])
    idx4 = np.stack([np.random.permutation(T)[:I] for _ in range(8)])
    fd = mx_kscale(D)
    keysp = pack_weight(n((D, T)) / fd[:, None], "e4m3")
    return {
        "query": (n((D, Q)) * 0.9 / np.sqrt(D) * fd[:, None]).astype(np.float32),
        "keys_words": keysp[0],
        "keys_scales": keysp[1],
        "lam": (np.random.uniform(0.7, 1.3, (Q, 1))).astype(np.float32),
        "old": (1.0 * n((Q, T))).astype(np.float32),
        "share2": (np.random.uniform(0.4, 1.2, (Q, 1))).astype(np.float32),
        "offs": striped8(idx),
        "offs2": striped8(idx2),
        "offs3": striped8(idx3),
        "offs4": striped8(idx4),
    }


def reference(query, keys_words, keys_scales, lam, old, share2, offs, offs2, offs3, offs4):
    idx = unstriped8(offs)
    idx2 = unstriped8(offs2)
    idx3 = unstriped8(offs3)
    idx4 = unstriped8(offs4)
    keysu = unpack_weight(keys_words, keys_scales, "e4m3")
    queryq = mxq(f64(query), 0, "e4m3")
    a = queryq.T @ keysu
    w = pick8(a, idx, 16) * f64(lam) - np.abs(pick8(a, idx2, 16) - pick8(a, idx3, 16))
    f1 = np.zeros((Q, T))
    f1[np.arange(Q)[:, None], idx[np.arange(Q) % 128 // 16]] = w
    f2 = np.zeros((Q, T))
    f2[np.arange(Q)[:, None], idx4[np.arange(Q) % 128 // 16]] = w
    y = f64(old) + f1 + f2 * f64(share2)
    return y

@@ -1,0 +1,148 @@
+from contextlib import ExitStack
+
+import concourse.mybir as mybir
+from concourse.masks import make_identity
+
+D, T, SLOTS, Q = 512, 1024, 512, 128
+FLOPS = 2 * D * T * Q
+
+F32 = mybir.dt.float32
+BF16 = mybir.dt.bfloat16
+I32 = mybir.dt.int32
+U32 = mybir.dt.uint32
+U16 = mybir.dt.uint16
+U8 = mybir.dt.uint8
+FP8X4 = mybir.dt.float8_e4m3fn_x4
+ALU = mybir.AluOpType
+ACT = mybir.ActivationFunctionType
+
+P = 128
+PACK = 4
+BANK = 512
+PIECE = 256
+HALF = SLOTS // 2
+HALF_COLS = HALF // 16
+
+
+def tile_attend_betweentwo_lean_twiceput_heads_kernel(
+    tc, query, keys_words, keys_scales, lam, old, share2, offs, offs2, offs3, offs4, out
+):
+    nc = tc.nc
+    with ExitStack() as ctx:
+        sb = ctx.enter_context(tc.tile_pool(name="sb", bufs=1))
+        ps = ctx.enter_context(tc.psum_pool(name="ps", bufs=1))
+
+        key_scale = sb.tile([P, T], U8, name="key_scale", align_bytes=64)
+        nc.vector.memset(key_scale[:].bitcast(U32), 0)
+
+        q_raw = sb.tile([P, PACK, Q], F32, name="q_raw")
+        nc.sync.dma_start(q_raw[:], query.rearrange("(p j) q -> p j q", j=PACK))
+        words = keys_words[0].rearrange("p n t -> p (n t)").bitcast(I32)
+        key_words = []
+        for h in range(T // BANK):
+            kw = sb.tile([P, BANK], U32, name="key_words%d" % h, align_bytes=64)
+            nc.sync.dma_start(kw[:].bitcast(I32), words[:, h * BANK : (h + 1) * BANK])
+            key_words.append(kw)
+        scale_rows = keys_scales[0].bitcast(I32)
+        for g in range(4):
+            nc.scalar.dma_start(key_scale[32 * g : 32 * g + 4, :].bitcast(I32), scale_rows[4 * g : 4 * g + 4, :])
+
+        lam_col = sb.tile([P, 1], F32, name="lam_col")
+        nc.sync.dma_start(lam_col[:], lam)
+        lists = []
+        for n, src in enumerate((offs2, offs, offs3, offs4)):
+            lt = sb.tile([P, SLOTS // 16], U16, name="list%d" % n)
+            nc.sync.dma_start(lt[:], src)
+            lists.append(lt)
+        list2, list1, list3, list4 = lists
+        old_sb = sb.tile([P, T], F32, name="old_sb")
+        nc.sync.dma_start(old_sb[:], old)
+        share_col = sb.tile([P, 1], F32, name="share_col")
+        nc.sync.dma_start(share_col[:], share2)
+
+        f1 = sb.tile([P, T], F32, name="f1")
+        f2 = sb.tile([P, T], F32, name="f2")
+        nc.vector.memset(f1[:], 0.0)
+        nc.vector.memset(f2[:], 0.0)
+        ident = sb.tile([P, P], F32, name="ident")
+        make_identity(nc, ident[:])
+
+        q_bf = sb.tile([P, Q, PACK], BF16, name="q_bf", align_bytes=64)
+        nc.vector.tensor_copy(q_bf[:], q_raw[:].rearrange("p j q -> p q j"))
+        q_words = sb.tile([P, Q], U32, name="q_words", align_bytes=64)
+        q_scale = sb.tile([P, Q], U8, name="q_scale", align_bytes=64)
+        nc.vector.quantize_mx(q_words[:].bitcast(FP8X4), q_scale[:], q_bf[:].rearrange("p q j -> p (q j)"))
+
+        lam_wide = sb.tile([P, HALF], F32, name="lam_wide")
+        nc.scalar.activation(lam_wide[:], lam_col[:].to_broadcast([P, HALF]), ACT.Copy)
+
+        a = sb.tile([P, T], F32, name="a")
+        for n in range(T // PIECE):
+            acc = ps.tile([P, PIECE], F32, name="acc%d" % n)
+            h, c = divmod(n * PIECE, BANK)
+            nc.tensor.matmul_mx(
+                acc[:],
+                lhsT=q_words[:].bitcast(FP8X4),
+                lhsT_scale=q_scale[:],
+                rhs=key_words[h][:, c : c + PIECE].bitcast(FP8X4),
+                rhs_scale=key_scale[:, n * PIECE : (n + 1) * PIECE],
+                start=True,
+                stop=True,
+            )
+            cols = slice(n * PIECE, (n + 1) * PIECE)
+            if n % 2 == 0:
+                nc.scalar.copy(a[:, cols], acc[:])
+            else:
+                nc.vector.tensor_copy(a[:, cols], acc[:])
+
+        first = sb.tile([P, SLOTS], F32, name="first")
+        first_raw = sb.tile([P, HALF], F32, name="first_raw")
+        second = sb.tile([P, SLOTS], F32, name="second")
+        diff = sb.tile([P, SLOTS], F32, name="diff")
+        dist = sb.tile([P, SLOTS], F32, name="dist")
+        minus = sb.tile([P, SLOTS], F32, name="minus")
+        sl = [slice(0, HALF), slice(HALF, SLOTS)]
+        lc = [slice(0, HALF_COLS), slice(HALF_COLS, 2 * HALF_COLS)]
+
+        for h in range(2):
+            nc.scalar.activation(second[:, sl[h]], a[:].indirect(list2[:, lc[h]]), ACT.Copy)
+        nc.vector.tensor_tensor(first[:, sl[0]], a[:].indirect(list1[:, lc[0]]), lam_wide[:], ALU.mult)
+        for h in range(2):
+            nc.vector.tensor_tensor(diff[:, sl[h]], a[:].indirect(list3[:, lc[h]]), second[:, sl[h]], ALU.subtract)
+        for h in range(2):
+            nc.scalar.activation(dist[:, sl[h]], diff[:, sl[h]], ACT.Abs)
+            nc.scalar.activation(minus[:, sl[h]], dist[:, sl[h]], ACT.Copy, scale=-1.0)
+        nc.scalar.activation(first_raw[:], a[:].indirect(list1[:, lc[1]]), ACT.Copy)
+        nc.scalar.activation(first[:, sl[1]], first_raw[:], ACT.Copy, scale=lam_col[:])
+
+        for h in range(2):
+            nc.vector.tensor_tensor(f1[:].indirect(list1[:, lc[h]]), first[:, sl[h]], minus[:, sl[h]], ALU.add)
+        nc.vector.tensor_tensor(f2[:].indirect(list4[:]), first[:], minus[:], ALU.add)
+
+        blocks = PIECE // P
+        pieces = T // PIECE
+        turned = []
+        for n in range(pieces):
+            tb = ps.tile([P, PIECE], F32, name="turned%d" % n)
+            for j in range(blocks):
+                cols = slice(n * PIECE + j * P, n * PIECE + (j + 1) * P)
+                nc.tensor.matmul(tb[:, j * P : (j + 1) * P], lhsT=old_sb[:, cols], rhs=ident[:], is_transpose=True, start=(j == 0), stop=False)
+            turned.append(tb)
+        turned_sb = []
+        for n in range(pieces):
+            tb = turned[n]
+            for j in range(blocks):
+                cols = slice(n * PIECE + j * P, n * PIECE + (j + 1) * P)
+                nc.tensor.matmul(tb[:, j * P : (j + 1) * P], lhsT=f1[:, cols], rhs=ident[:], is_transpose=True, start=False, stop=(j == blocks - 1))
+            ts = sb.tile([P, PIECE], F32, name="turned_sb%d" % n)
+            nc.scalar.copy(ts[:], tb[:])
+            turned_sb.append(ts)
+        for n in range(pieces):
+            pb = ps.tile([P, PIECE], F32, name="acc%d" % n)
+            for j in range(blocks):
+                nc.tensor.transpose(pb[:, j * P : (j + 1) * P], turned_sb[n][:, j * P : (j + 1) * P], ident[:])
+            cols = slice(n * PIECE, (n + 1) * PIECE)
+            res = sb.tile([P, PIECE], F32, name="res%d" % n)
+            nc.vector.scalar_tensor_tensor(res[:], f2[:, cols], share_col[:], pb[:], ALU.mult, ALU.add)
+            eng = nc.sync if n % 2 == 0 else nc.scalar
+            eng.dma_start(out[:, cols], res[:])

@@ -41,14 +41,15 @@ def tile_attend_betweentwo_lean_twiceput_heads_kernel(
         key_words = []
         for h in range(T // BANK):
             kw = sb.tile([P, BANK], U32, name="key_words%d" % h, align_bytes=64)
-            nc.sync.dma_start(kw[:].bitcast(I32), words[:, h * BANK : (h + 1) * BANK])
             key_words.append(kw)
+        nc.sync.dma_start(key_words[0][:].bitcast(I32), words[:, :BANK])
         scale_rows = keys_scales[0].bitcast(I32)
         for g in range(4):
-            nc.scalar.dma_start(key_scale[32 * g : 32 * g + 4, :].bitcast(I32), scale_rows[4 * g : 4 * g + 4, :])
+            nc.sync.dma_start(key_scale[32 * g : 32 * g + 4, :].bitcast(I32), scale_rows[4 * g : 4 * g + 4, :])
+        nc.sync.dma_start(key_words[1][:].bitcast(I32), words[:, BANK:])
 
         lam_col = sb.tile([P, 1], F32, name="lam_col")
-        nc.sync.dma_start(lam_col[:], lam)
+        nc.scalar.dma_start(lam_col[:], lam)
         lists = []
         for n, src in enumerate((offs2, offs, offs3, offs4)):
             lt = sb.tile([P, SLOTS // 16], U16, name="list%d" % n)
@@ -60,47 +61,50 @@ def tile_attend_betweentwo_lean_twiceput_heads_kernel(
         share_col = sb.tile([P, 1], F32, name="share_col")
         nc.sync.dma_start(share_col[:], share2)
 
-        f1 = sb.tile([P, T], F32, name="f1")
+        f1 = [sb.tile([P, T], F32, name="f1a")]
         f2 = sb.tile([P, T], F32, name="f2")
-        nc.vector.memset(f1[:], 0.0)
+        nc.vector.memset(f1[0][:], 0.0)
         nc.vector.memset(f2[:], 0.0)
         ident = sb.tile([P, P], F32, name="ident")
         make_identity(nc, ident[:])
 
-        q_bf = sb.tile([P, Q, PACK], BF16, name="q_bf", align_bytes=64)
+        q_bf = sb.tile([P, Q, PACK], BF16, name="q_bf", tag="early", align_bytes=64)
         nc.vector.tensor_copy(q_bf[:], q_raw[:].rearrange("p j q -> p q j"))
         q_words = sb.tile([P, Q], U32, name="q_words", align_bytes=64)
         q_scale = sb.tile([P, Q], U8, name="q_scale", align_bytes=64)
         nc.vector.quantize_mx(q_words[:].bitcast(FP8X4), q_scale[:], q_bf[:].rearrange("p q j -> p (q j)"))
 
+        f1.append(sb.tile([P, T], F32, name="f1b", tag="early", align_bytes=64))
+        nc.vector.memset(f1[1][:], 0.0)
         lam_wide = sb.tile([P, HALF], F32, name="lam_wide")
-        nc.scalar.activation(lam_wide[:], lam_col[:].to_broadcast([P, HALF]), ACT.Copy)
+        nc.scalar.activation(lam_wide[:], lam_col[:].to_broadcast([P, HALF]), ACT.Copy, scale=-1.0)
 
         a = sb.tile([P, T], F32, name="a")
-        for n in range(T // PIECE):
-            acc = ps.tile([P, PIECE], F32, name="acc%d" % n)
-            h, c = divmod(n * PIECE, BANK)
+        widths = (256, 256, 256, 128, 128)
+        start = 0
+        for n, width in enumerate(widths):
+            acc = ps.tile([P, width], F32, name="acc%d" % n, tag="bank%d" % n)
+            h, c = divmod(start, BANK)
+            cols = slice(start, start + width)
             nc.tensor.matmul_mx(
                 acc[:],
                 lhsT=q_words[:].bitcast(FP8X4),
                 lhsT_scale=q_scale[:],
-                rhs=key_words[h][:, c : c + PIECE].bitcast(FP8X4),
-                rhs_scale=key_scale[:, n * PIECE : (n + 1) * PIECE],
+                rhs=key_words[h][:, c : c + width].bitcast(FP8X4),
+                rhs_scale=key_scale[:, cols],
                 start=True,
                 stop=True,
             )
-            cols = slice(n * PIECE, (n + 1) * PIECE)
-            if n % 2 == 0:
+            if n % 2 == 1:
                 nc.scalar.copy(a[:, cols], acc[:])
             else:
                 nc.vector.tensor_copy(a[:, cols], acc[:])
+            start = start + width
 
         first = sb.tile([P, SLOTS], F32, name="first")
-        first_raw = sb.tile([P, HALF], F32, name="first_raw")
         second = sb.tile([P, SLOTS], F32, name="second")
-        diff = sb.tile([P, SLOTS], F32, name="diff")
+        diff = sb.tile([P, SLOTS], F32, name="diff", tag="late")
         dist = sb.tile([P, SLOTS], F32, name="dist")
-        minus = sb.tile([P, SLOTS], F32, name="minus")
         sl = [slice(0, HALF), slice(HALF, SLOTS)]
         lc = [slice(0, HALF_COLS), slice(HALF_COLS, 2 * HALF_COLS)]
 
@@ -109,40 +113,49 @@ def tile_attend_betweentwo_lean_twiceput_heads_kernel(
         nc.vector.tensor_tensor(first[:, sl[0]], a[:].indirect(list1[:, lc[0]]), lam_wide[:], ALU.mult)
         for h in range(2):
             nc.vector.tensor_tensor(diff[:, sl[h]], a[:].indirect(list3[:, lc[h]]), second[:, sl[h]], ALU.subtract)
-        for h in range(2):
-            nc.scalar.activation(dist[:, sl[h]], diff[:, sl[h]], ACT.Abs)
-            nc.scalar.activation(minus[:, sl[h]], dist[:, sl[h]], ACT.Copy, scale=-1.0)
-        nc.scalar.activation(first_raw[:], a[:].indirect(list1[:, lc[1]]), ACT.Copy)
-        nc.scalar.activation(first[:, sl[1]], first_raw[:], ACT.Copy, scale=lam_col[:])
+        nc.scalar.activation(dist[:, sl[0]], diff[:, sl[0]], ACT.Abs)
+        nc.scalar.activation(diff[:, sl[0]], a[:].indirect(list1[:, lc[1]]), ACT.Copy)
+        nc.scalar.activation(dist[:, sl[1]], diff[:, sl[1]], ACT.Abs)
+        nc.scalar.activation(first[:, sl[1]], diff[:, sl[0]], ACT.Copy, scale=lam_wide[:, 0:1])
 
         for h in range(2):
-            nc.vector.tensor_tensor(f1[:].indirect(list1[:, lc[h]]), first[:, sl[h]], minus[:, sl[h]], ALU.add)
-        nc.vector.tensor_tensor(f2[:].indirect(list4[:]), first[:], minus[:], ALU.add)
+            nc.vector.tensor_tensor(f1[h][:].indirect(list1[:, lc[h]]), first[:, sl[h]], dist[:, sl[h]], ALU.add)
+        nc.vector.tensor_tensor(f2[:].indirect(list4[:]), first[:], dist[:], ALU.add)
 
+        minus_share = sb.tile([P, 1], F32, name="minus_share")
+        nc.scalar.activation(minus_share[:], share_col[:], ACT.Copy, scale=-1.0)
+        minus_old = sb.tile([P, T], F32, name="minus_old", tag="late")
         blocks = PIECE // P
         pieces = T // PIECE
         turned = []
         for n in range(pieces):
-            tb = ps.tile([P, PIECE], F32, name="turned%d" % n)
-            for j in range(blocks):
-                cols = slice(n * PIECE + j * P, n * PIECE + (j + 1) * P)
-                nc.tensor.matmul(tb[:, j * P : (j + 1) * P], lhsT=old_sb[:, cols], rhs=ident[:], is_transpose=True, start=(j == 0), stop=False)
-            turned.append(tb)
+            cols = slice(n * PIECE, (n + 1) * PIECE)
+            nc.scalar.activation(minus_old[:, cols], old_sb[:, cols], ACT.Copy, scale=-1.0)
+            turned.append(ps.tile([P, PIECE], F32, name="turned%d" % n, tag="bank%d" % n))
+        terms = (f1[0], minus_old, f1[1])
+        for k, term in enumerate(terms):
+            for n in range(pieces):
+                for j in range(blocks):
+                    cols = slice(n * PIECE + j * P, n * PIECE + (j + 1) * P)
+                    nc.tensor.matmul(
+                        turned[n][:, j * P : (j + 1) * P],
+                        lhsT=term[:, cols],
+                        rhs=ident[:],
+                        is_transpose=True,
+                        start=(k == 0 and j == 0),
+                        stop=(k == len(terms) - 1 and j == blocks - 1),
+                    )
         turned_sb = []
         for n in range(pieces):
-            tb = turned[n]
-            for j in range(blocks):
-                cols = slice(n * PIECE + j * P, n * PIECE + (j + 1) * P)
-                nc.tensor.matmul(tb[:, j * P : (j + 1) * P], lhsT=f1[:, cols], rhs=ident[:], is_transpose=True, start=False, stop=(j == blocks - 1))
             ts = sb.tile([P, PIECE], F32, name="turned_sb%d" % n)
-            nc.scalar.copy(ts[:], tb[:])
+            nc.scalar.activation(ts[:], turned[n][:], ACT.Copy, scale=-1.0)
             turned_sb.append(ts)
         for n in range(pieces):
-            pb = ps.tile([P, PIECE], F32, name="acc%d" % n)
+            pb = ps.tile([P, PIECE], F32, name="back%d" % n, tag="bank%d" % (pieces + n))
             for j in range(blocks):
                 nc.tensor.transpose(pb[:, j * P : (j + 1) * P], turned_sb[n][:, j * P : (j + 1) * P], ident[:])
             cols = slice(n * PIECE, (n + 1) * PIECE)
             res = sb.tile([P, PIECE], F32, name="res%d" % n)
-            nc.vector.scalar_tensor_tensor(res[:], f2[:, cols], share_col[:], pb[:], ALU.mult, ALU.add)
+            nc.vector.scalar_tensor_tensor(res[:], f2[:, cols], minus_share[:], pb[:], ALU.mult, ALU.add)
             eng = nc.sync if n % 2 == 0 else nc.scalar
             eng.dma_start(out[:, cols], res[:])

@@ -49,7 +49,7 @@ def tile_attend_betweentwo_lean_twiceput_heads_kernel(
         nc.sync.dma_start(key_words[1][:].bitcast(I32), words[:, BANK:])
 
         lam_col = sb.tile([P, 1], F32, name="lam_col")
-        nc.scalar.dma_start(lam_col[:], lam)
+        nc.gpsimd.dma_start(lam_col[:], lam)
         lists = []
         for n, src in enumerate((offs2, offs, offs3, offs4)):
             lt = sb.tile([P, SLOTS // 16], U16, name="list%d" % n)
@@ -59,7 +59,7 @@ def tile_attend_betweentwo_lean_twiceput_heads_kernel(
         old_sb = sb.tile([P, T], F32, name="old_sb")
         nc.sync.dma_start(old_sb[:], old)
         share_col = sb.tile([P, 1], F32, name="share_col")
-        nc.sync.dma_start(share_col[:], share2)
+        nc.gpsimd.dma_start(share_col[:], share2)
 
         f1 = [sb.tile([P, T], F32, name="f1a")]
         f2 = sb.tile([P, T], F32, name="f2")
@@ -69,7 +69,9 @@ def tile_attend_betweentwo_lean_twiceput_heads_kernel(
         make_identity(nc, ident[:])
 
         q_bf = sb.tile([P, Q, PACK], BF16, name="q_bf", tag="early", align_bytes=64)
-        nc.vector.tensor_copy(q_bf[:], q_raw[:].rearrange("p j q -> p q j"))
+        q_turned = q_raw[:].rearrange("p j q -> p q j")
+        nc.vector.tensor_copy(q_bf[:, :96, :], q_turned[:, :96, :])
+        nc.scalar.copy(q_bf[:, 96:, :], q_turned[:, 96:, :])
         q_words = sb.tile([P, Q], U32, name="q_words", align_bytes=64)
         q_scale = sb.tile([P, Q], U8, name="q_scale", align_bytes=64)
         nc.vector.quantize_mx(q_words[:].bitcast(FP8X4), q_scale[:], q_bf[:].rearrange("p q j -> p (q j)"))
@@ -95,7 +97,7 @@ def tile_attend_betweentwo_lean_twiceput_heads_kernel(
                 start=True,
                 stop=True,
             )
-            if n % 2 == 1:
+            if n in (0, 1, 3):
                 nc.scalar.copy(a[:, cols], acc[:])
             else:
                 nc.vector.tensor_copy(a[:, cols], acc[:])
@@ -123,7 +125,7 @@ def tile_attend_betweentwo_lean_twiceput_heads_kernel(
         nc.vector.tensor_tensor(f2[:].indirect(list4[:]), first[:], dist[:], ALU.add)
 
         minus_share = sb.tile([P, 1], F32, name="minus_share")
-        nc.scalar.activation(minus_share[:], share_col[:], ACT.Copy, scale=-1.0)
+        nc.gpsimd.tensor_scalar(minus_share[:], share_col[:], -1.0, 0.0, ALU.mult, ALU.add)
         minus_old = sb.tile([P, T], F32, name="minus_old", tag="late")
         blocks = PIECE // P
         pieces = T // PIECE

from contextlib import ExitStack

import concourse.mybir as mybir
from concourse.masks import make_identity

D, T, SLOTS, Q = 512, 1024, 512, 128
FLOPS = 2 * D * T * Q

F32 = mybir.dt.float32
BF16 = mybir.dt.bfloat16
I32 = mybir.dt.int32
U32 = mybir.dt.uint32
U16 = mybir.dt.uint16
U8 = mybir.dt.uint8
FP8X4 = mybir.dt.float8_e4m3fn_x4
ALU = mybir.AluOpType
ACT = mybir.ActivationFunctionType

P = 128
PACK = 4
BANK = 512
PIECE = 256
HALF = SLOTS // 2
HALF_COLS = HALF // 16


def tile_attend_betweentwo_lean_twiceput_heads_kernel(
    tc, query, keys_words, keys_scales, lam, old, share2, offs, offs2, offs3, offs4, out
):
    nc = tc.nc
    with ExitStack() as ctx:
        sb = ctx.enter_context(tc.tile_pool(name="sb", bufs=1))
        ps = ctx.enter_context(tc.psum_pool(name="ps", bufs=1))

        key_scale = sb.tile([P, T], U8, name="key_scale", align_bytes=64)
        nc.vector.memset(key_scale[:].bitcast(U32), 0)

        q_raw = sb.tile([P, PACK, Q], F32, name="q_raw")
        nc.sync.dma_start(q_raw[:], query.rearrange("(p j) q -> p j q", j=PACK))
        words = keys_words[0].rearrange("p n t -> p (n t)").bitcast(I32)
        key_words = []
        for h in range(T // BANK):
            kw = sb.tile([P, BANK], U32, name="key_words%d" % h, align_bytes=64)
            key_words.append(kw)
        nc.sync.dma_start(key_words[0][:].bitcast(I32), words[:, :BANK])
        scale_rows = keys_scales[0].bitcast(I32)
        for g in range(4):
            nc.sync.dma_start(key_scale[32 * g : 32 * g + 4, :].bitcast(I32), scale_rows[4 * g : 4 * g + 4, :])
        nc.sync.dma_start(key_words[1][:].bitcast(I32), words[:, BANK:])

        lam_col = sb.tile([P, 1], F32, name="lam_col")
        nc.gpsimd.dma_start(lam_col[:], lam)
        lists = []
        for n, src in enumerate((offs2, offs, offs3, offs4)):
            lt = sb.tile([P, SLOTS // 16], U16, name="list%d" % n)
            nc.sync.dma_start(lt[:], src)
            lists.append(lt)
        list2, list1, list3, list4 = lists
        old_sb = sb.tile([P, T], F32, name="old_sb")
        nc.sync.dma_start(old_sb[:], old)
        share_col = sb.tile([P, 1], F32, name="share_col")
        nc.gpsimd.dma_start(share_col[:], share2)

        f1 = [sb.tile([P, T], F32, name="f1a")]
        f2 = sb.tile([P, T], F32, name="f2")
        nc.vector.memset(f1[0][:], 0.0)
        nc.vector.memset(f2[:], 0.0)
        ident = sb.tile([P, P], F32, name="ident")
        make_identity(nc, ident[:])

        q_bf = sb.tile([P, Q, PACK], BF16, name="q_bf", tag="early", align_bytes=64)
        q_turned = q_raw[:].rearrange("p j q -> p q j")
        nc.vector.tensor_copy(q_bf[:, :96, :], q_turned[:, :96, :])
        nc.scalar.copy(q_bf[:, 96:, :], q_turned[:, 96:, :])
        q_words = sb.tile([P, Q], U32, name="q_words", align_bytes=64)
        q_scale = sb.tile([P, Q], U8, name="q_scale", align_bytes=64)
        nc.vector.quantize_mx(q_words[:].bitcast(FP8X4), q_scale[:], q_bf[:].rearrange("p q j -> p (q j)"))

        f1.append(sb.tile([P, T], F32, name="f1b", tag="early", align_bytes=64))
        nc.vector.memset(f1[1][:], 0.0)
        lam_wide = sb.tile([P, HALF], F32, name="lam_wide")
        nc.scalar.activation(lam_wide[:], lam_col[:].to_broadcast([P, HALF]), ACT.Copy, scale=-1.0)

        a = sb.tile([P, T], F32, name="a")
        widths = (256, 256, 256, 128, 128)
        start = 0
        for n, width in enumerate(widths):
            acc = ps.tile([P, width], F32, name="acc%d" % n, tag="bank%d" % n)
            h, c = divmod(start, BANK)
            cols = slice(start, start + width)
            nc.tensor.matmul_mx(
                acc[:],
                lhsT=q_words[:].bitcast(FP8X4),
                lhsT_scale=q_scale[:],
                rhs=key_words[h][:, c : c + width].bitcast(FP8X4),
                rhs_scale=key_scale[:, cols],
                start=True,
                stop=True,
            )
            if n in (0, 1, 3):
                nc.scalar.copy(a[:, cols], acc[:])
            else:
                nc.vector.tensor_copy(a[:, cols], acc[:])
            start = start + width

        first = sb.tile([P, SLOTS], F32, name="first")
        second = sb.tile([P, SLOTS], F32, name="second")
        diff = sb.tile([P, SLOTS], F32, name="diff", tag="late")
        dist = sb.tile([P, SLOTS], F32, name="dist")
        sl = [slice(0, HALF), slice(HALF, SLOTS)]
        lc = [slice(0, HALF_COLS), slice(HALF_COLS, 2 * HALF_COLS)]

        for h in range(2):
            nc.scalar.activation(second[:, sl[h]], a[:].indirect(list2[:, lc[h]]), ACT.Copy)
        nc.vector.tensor_tensor(first[:, sl[0]], a[:].indirect(list1[:, lc[0]]), lam_wide[:], ALU.mult)
        for h in range(2):
            nc.vector.tensor_tensor(diff[:, sl[h]], a[:].indirect(list3[:, lc[h]]), second[:, sl[h]], ALU.subtract)
        nc.scalar.activation(dist[:, sl[0]], diff[:, sl[0]], ACT.Abs)
        nc.scalar.activation(diff[:, sl[0]], a[:].indirect(list1[:, lc[1]]), ACT.Copy)
        nc.scalar.activation(dist[:, sl[1]], diff[:, sl[1]], ACT.Abs)
        nc.scalar.activation(first[:, sl[1]], diff[:, sl[0]], ACT.Copy, scale=lam_wide[:, 0:1])

        for h in range(2):
            nc.vector.tensor_tensor(f1[h][:].indirect(list1[:, lc[h]]), first[:, sl[h]], dist[:, sl[h]], ALU.add)
        nc.vector.tensor_tensor(f2[:].indirect(list4[:]), first[:], dist[:], ALU.add)

        minus_share = sb.tile([P, 1], F32, name="minus_share")
        nc.gpsimd.tensor_scalar(minus_share[:], share_col[:], -1.0, 0.0, ALU.mult, ALU.add)
        minus_old = sb.tile([P, T], F32, name="minus_old", tag="late")
        blocks = PIECE // P
        pieces = T // PIECE
        turned = []
        for n in range(pieces):
            cols = slice(n * PIECE, (n + 1) * PIECE)
            nc.scalar.activation(minus_old[:, cols], old_sb[:, cols], ACT.Copy, scale=-1.0)
            turned.append(ps.tile([P, PIECE], F32, name="turned%d" % n, tag="bank%d" % n))
        terms = (f1[0], minus_old, f1[1])
        for k, term in enumerate(terms):
            for n in range(pieces):
                for j in range(blocks):
                    cols = slice(n * PIECE + j * P, n * PIECE + (j + 1) * P)
                    nc.tensor.matmul(
                        turned[n][:, j * P : (j + 1) * P],
                        lhsT=term[:, cols],
                        rhs=ident[:],
                        is_transpose=True,
                        start=(k == 0 and j == 0),
                        stop=(k == len(terms) - 1 and j == blocks - 1),
                    )
        turned_sb = []
        for n in range(pieces):
            ts = sb.tile([P, PIECE], F32, name="turned_sb%d" % n)
            nc.scalar.activation(ts[:], turned[n][:], ACT.Copy, scale=-1.0)
            turned_sb.append(ts)
        for n in range(pieces):
            pb = ps.tile([P, PIECE], F32, name="back%d" % n, tag="bank%d" % (pieces + n))
            for j in range(blocks):
                nc.tensor.transpose(pb[:, j * P : (j + 1) * P], turned_sb[n][:, j * P : (j + 1) * P], ident[:])
            cols = slice(n * PIECE, (n + 1) * PIECE)
            res = sb.tile([P, PIECE], F32, name="res%d" % n)
            nc.vector.scalar_tensor_tensor(res[:], f2[:, cols], minus_share[:], pb[:], ALU.mult, ALU.add)
            eng = nc.sync if n % 2 == 0 else nc.scalar
            eng.dma_start(out[:, cols], res[:])
